import numpy as np
import ml_dtypes


def mxq(x, axis, fmt="e4m3"):
    dtype, down = {"e4m3": (ml_dtypes.float8_e4m3fn, 7), "e5m2": (ml_dtypes.float8_e5m2, 14)}[fmt]
    v = np.moveaxis(np.asarray(x, np.float32).astype(ml_dtypes.bfloat16).astype(np.float64), axis, -1)
    blocks = v.reshape(v.shape[:-1] + (-1, 32))
    amax = np.abs(blocks).max(-1, keepdims=True)
    byte = np.maximum(np.where(amax > 0, np.frexp(amax)[1] - 1 + 127, 0) - down, 1)
    scale = np.exp2(byte - 127.0)
    codes = (blocks / scale).astype(np.float32).astype(dtype).astype(np.float64)
    return np.moveaxis((codes * scale).reshape(v.shape), -1, axis)


WIDE = False


def mx_kscale(k):
    if not WIDE:
        return np.ones(k)
    levels = np.array([10, -10, 5, -5, 0])
    if k % 512:
        return np.exp2(np.random.permutation(np.resize(levels, k // 32))).repeat(32)
    a = np.empty((k // 512, 16))
    for p in range(k // 512):
        a[p, :8] = np.random.permutation(np.resize(levels, 8))
        for g in range(8):
            far = levels[np.abs(levels - a[p, g]) >= 10]
            a[p, g + 8] = far[np.random.randint(len(far))]
    return np.exp2(a.ravel()).repeat(32)


def f64(x):
    return np.asarray(x).astype(np.float64)


def striped(idx):
    return np.tile(idx.reshape(-1, 16).T, (8, 1)).astype(np.uint16)


def unstriped(offs):
    return offs[:16].T.reshape(-1).astype(np.int64)


def striped8(idx):
    return np.concatenate([x.reshape(-1, 16).T for x in idx]).astype(np.uint16)


def runs(offs, k):
    lists = np.stack([offs[16 * r : 16 * r + 16].T.reshape(-1) for r in range(8)]).astype(np.int64)
    return lists[np.arange(k) % 512 // 64]


def pack_weight(w):
    k, n = w.shape
    w = f64(np.asarray(w, np.float32).astype(ml_dtypes.bfloat16)).reshape(k // 32, 32, n)
    amax = np.abs(w).max(1)
    byte = np.clip(np.where(amax > 0, np.frexp(amax)[1] - 1 + 127 - 7, 1), 1, 254)
    scaled = (w * np.exp2(127.0 - byte)[:, None, :]).reshape(k, n).astype(np.float32)
    words = np.ascontiguousarray(scaled.reshape(k // 512, 128, 4, n).transpose(0, 1, 3, 2)).astype(ml_dtypes.float8_e4m3fn).view(np.uint8)
    return words, np.ascontiguousarray(byte.astype(np.uint8).reshape(k // 512, 16, n))


def unpack_weight(words, scales):
    g, p, n, _ = words.shape
    vals = np.ascontiguousarray(words).view(ml_dtypes.float8_e4m3fn).astype(np.float64) * np.repeat(np.exp2(scales.astype(np.float64) - 127.0), 8, axis=1)[..., None]
    return vals.transpose(0, 1, 3, 2).reshape(g * 512, n)


K, T, S, N, G, H, W = 512, 1024, 256, 512, 2048, 512, 128


def setup_inputs():
    n = np.random.standard_normal
    s = mx_kscale(K)[:, None]
    u = mx_kscale(K)
    packed_xT = pack_weight(n((K, T)) * s)
    packed_dT = pack_weight(n((K, G)) / s)
    packed_w1 = pack_weight(n((H, N)) / np.sqrt(2 * H) / u[:, None])
    packed_w2 = pack_weight(n((K, N)) / np.sqrt(2 * K) / s)
    perm = np.random.permutation(S)
    return {
        "x_words": packed_xT[0],
        "x_scales": packed_xT[1],
        "d_words": packed_dT[0],
        "d_scales": packed_dT[1],
        "gn": (np.random.uniform(0.5, 1.5, (H, 1)) * u[:, None]).astype(np.float32),
        "w1_words": packed_w1[0],
        "w1_scales": packed_w1[1],
        "w2_words": packed_w2[0],
        "w2_scales": packed_w2[1],
        "offs": striped8(np.random.randint(0, T, (8, S))),
        "ci": striped(np.random.permutation(G)[:H]),
        "n1": striped(np.random.permutation(S)),
        "n2": striped(np.random.permutation(S)),
        "n3": striped(np.random.permutation(S)),
        "hz": striped8(np.random.randint(0, T, (8, S))),
        "n4": striped(perm[:W]),
        "n5": striped(perm[W:]),
    }


def reference(x_words, x_scales, d_words, d_scales, gn, w1_words, w1_scales, w2_words, w2_scales, offs, ci, n1, n2, n3, hz, n4, n5):
    d_ci = unpack_weight(d_words, d_scales)[:, unstriped(ci)]
    xq = unpack_weight(x_words, x_scales)[np.arange(K)[:, None], runs(offs, K)]
    s = 0.0625 * (d_ci.T @ xq)
    ds = np.zeros((H, S))
    ds[:, unstriped(n1)] = s
    st = np.minimum(ds, s[:, unstriped(n2)])
    z = f64(gn) * (st - st[:, unstriped(n3)])
    x_hz = unpack_weight(x_words, x_scales)[np.arange(K)[:, None], runs(hz, K)]
    h2 = unpack_weight(w1_words, w1_scales).T @ mxq(z, 0, "e4m3") + unpack_weight(w2_words, w2_scales).T @ x_hz
    pb = h2[:, unstriped(n5)]
    pa = h2[:, unstriped(n4)]
    rb = pb - (0.5 * pa)
    ra = np.sqrt((pa) ** 2 + (pb) ** 2 + 0.25)
    ua = np.zeros((N, S))
    ua[:, unstriped(n4)] = ra
    out = ua.copy()
    out[:, unstriped(n5)] = rb
    return out

@@ -1,0 +1,204 @@
+from contextlib import ExitStack
+
+import concourse.mybir as mybir
+
+K, T, S, N, G, H, W = 512, 1024, 256, 512, 2048, 512, 128
+FLOPS = 3 * 2 * 512 * 512 * 256
+
+F32 = mybir.dt.float32
+BF16 = mybir.dt.bfloat16
+I32 = mybir.dt.int32
+U32 = mybir.dt.uint32
+U16 = mybir.dt.uint16
+U8 = mybir.dt.uint8
+FP8X4 = mybir.dt.float8_e4m3fn_x4
+ALU = mybir.AluOpType
+ACT = mybir.ActivationFunctionType
+
+P = 128
+PACK = 4
+HALF = S // 2
+GATHER_COLS = S + 8
+SCATTER_COLS = S + 96
+
+
+def tile_picked_xhznhsndminpolar_none_p_kernel(
+    tc, x_words, x_scales, d_words, d_scales, gn, w1_words, w1_scales, w2_words, w2_scales,
+    offs, ci, n1, n2, n3, hz, n4, n5, out,
+):
+    nc = tc.nc
+
+    def words_of(table):
+        return table[0].rearrange("p n r -> p (n r)").bitcast(I32)
+
+    with ExitStack() as ctx:
+        lists = ctx.enter_context(tc.tile_pool(name="lists", bufs=1))
+        keep = ctx.enter_context(tc.tile_pool(name="keep", bufs=1))
+        psum = ctx.enter_context(tc.psum_pool(name="psum", bufs=1))
+
+        def load_list(source, name):
+            tile = lists.tile(list(source.shape), U16, name=name)
+            nc.sync.dma_start(tile[:], source)
+            return tile
+
+        x_bytes = keep.tile([P, T], U8, name="x_bytes", align_bytes=64)
+        d_bytes = keep.tile([P, G], U8, name="d_bytes", align_bytes=64)
+
+        def load_scale_rows(tile, scales):
+            rows = scales[0].bitcast(I32)
+            nc.sync.dma_start(tile[:].bitcast(I32), rows.unsqueeze(1).to_broadcast([16, 8, rows.shape[1]]))
+
+        offs_list = load_list(offs, "offs_list")
+        load_scale_rows(x_bytes, x_scales)
+        ci_list = load_list(ci, "ci_list")
+        load_scale_rows(d_bytes, d_scales)
+        n1_list = load_list(n1, "n1_list")
+        n2_list = load_list(n2, "n2_list")
+        n3_list = load_list(n3, "n3_list")
+        d_table = keep.tile([P, G], U32, name="d_table", tag="big_words", align_bytes=64)
+        nc.sync.dma_start(d_table[:].bitcast(I32), words_of(d_words))
+        x_table = keep.tile([P, T], U32, name="x_table", align_bytes=64)
+        nc.sync.dma_start(x_table[:].bitcast(I32), words_of(x_words))
+        hz_list = load_list(hz, "hz_list")
+        n4_list = load_list(n4, "n4_list")
+        n5_list = load_list(n5, "n5_list")
+        gain = keep.tile([P, PACK], F32, name="gain")
+        nc.gpsimd.dma_start(gain[:], gn.rearrange("(p t) o -> p (t o)", t=PACK))
+
+        def move_scale_rows(queue, planes, picked):
+            for r in range(4):
+                queue.dma_start(planes[r:P:32, :].bitcast(I32), picked[8 * r : P : 32, :].bitcast(I32))
+
+        s_planes = keep.tile([P, H + S], U8, name="s_planes", align_bytes=64)
+        nc.gpsimd.memset(s_planes[:].bitcast(I32), 0)
+        hz_planes = keep.tile([P, S], U8, name="hz_planes", align_bytes=64)
+        nc.gpsimd.memset(hz_planes[:].bitcast(I32), 0)
+        s_picked = keep.tile([P, H + S], U8, name="s_picked", tag="picked_bytes", align_bytes=64)
+        nc.vector.tensor_copy(s_picked[:, H:], x_bytes[:].indirect(offs_list[:]))
+        nc.vector.tensor_copy(s_picked[:, :H].rearrange("p (t m) -> p m t", t=PACK), d_bytes[:].indirect(ci_list[:]))
+        move_scale_rows(nc.scalar, s_planes, s_picked)
+
+        d_codes = keep.tile([P, H], U32, name="d_codes", align_bytes=64)
+        nc.vector.tensor_copy(d_codes[:].rearrange("p (t m) -> p m t", t=PACK), d_table[:].indirect(ci_list[:]))
+        x_codes = keep.tile([P, S], U32, name="x_codes", align_bytes=64)
+        nc.vector.tensor_copy(x_codes[:], x_table[:].indirect(offs_list[:]))
+
+        scores = [keep.tile([P, GATHER_COLS], F32, name="scores%d" % t) for t in range(PACK)]
+        for t in range(PACK):
+            nc.gpsimd.memset(scores[t][:, S:], 0.0)
+            bank = psum.tile([P, S], F32, name="s_bank%d" % t, tag="bank%d" % t)
+            cols = slice(P * t, P * (t + 1))
+            nc.tensor.matmul_mx(
+                bank[:], lhsT=d_codes[:, cols].bitcast(FP8X4), lhsT_scale=s_planes[:, cols],
+                rhs=x_codes[:].bitcast(FP8X4), rhs_scale=s_planes[:, H:], start=True, stop=True,
+            )
+            nc.vector.tensor_scalar(scores[t][:, :S], bank[:], 0.0625, None, ALU.mult)
+
+        w_codes = keep.tile([P, 2, N], U32, name="w_codes", tag="big_words", align_bytes=64)
+        w_planes = keep.tile([P, 2, N], U8, name="w_planes", tag="picked_bytes", align_bytes=64)
+        nc.gpsimd.memset(w_planes[:].rearrange("p a n -> p (a n)").bitcast(I32), 0)
+        for a, (words, scales) in enumerate(((w2_words, w2_scales), (w1_words, w1_scales))):
+            nc.sync.dma_start(w_codes[:, a, :].bitcast(I32), words_of(words))
+            for q in range(4):
+                nc.sync.dma_start(
+                    w_planes[32 * q : 32 * q + 4, a, :].bitcast(I32), scales[0, 4 * q : 4 * q + 4, :].bitcast(I32)
+                )
+
+        hz_picked = keep.tile([P, S], U8, name="hz_picked", align_bytes=64)
+        nc.vector.tensor_copy(hz_picked[:], x_bytes[:].indirect(hz_list[:]))
+        move_scale_rows(nc.sync, hz_planes, hz_picked)
+        hz_codes = keep.tile([P, S], U32, name="hz_codes", align_bytes=64)
+        nc.vector.tensor_copy(hz_codes[:], x_table[:].indirect(hz_list[:]))
+
+        gained = keep.tile([P, PACK, S], F32, name="gained")
+        for t in range(PACK):
+            sent = keep.tile([P, SCATTER_COLS], F32, name="sent%d" % t)
+            nc.scalar.activation(sent[:].indirect(n1_list[:]), scores[t][:, :S], ACT.Copy)
+            fetched = keep.tile([P, S], F32, name="fetched%d" % t)
+            nc.scalar.activation(fetched[:], scores[t][:].indirect(n2_list[:]), ACT.Copy)
+            least = keep.tile([P, S], F32, name="least%d" % t)
+            nc.vector.tensor_tensor(least[:], sent[:, :S], fetched[:], ALU.min)
+            nc.vector.tensor_scalar(gained[:, t, :], least[:], gain[:, t : t + 1], None, ALU.mult)
+
+        h_banks = [
+            [psum.tile([P, HALF], F32, name="h_bank%d_%d" % (half, m), tag="bank%d" % (4 * (1 - half) + m)) for m in range(N // P)]
+            for half in range(2)
+        ]
+        for half in range(2):
+            places = slice(HALF * half, HALF * (half + 1))
+            for m in range(N // P):
+                cols = slice(P * m, P * (m + 1))
+                nc.tensor.matmul_mx(
+                    h_banks[half][m][:], lhsT=w_codes[:, 0, cols].bitcast(FP8X4), lhsT_scale=w_planes[:, 0, cols],
+                    rhs=hz_codes[:, places].bitcast(FP8X4), rhs_scale=hz_planes[:, places], start=True, stop=False,
+                )
+
+        partner = keep.tile([P, PACK, S], F32, name="partner")
+        z_rounded = keep.tile([P, S, PACK], BF16, name="z_rounded", align_bytes=64)
+        z_codes = keep.tile([P, S], U32, name="z_codes", align_bytes=64)
+        z_planes = keep.tile([P, S], U8, name="z_planes", align_bytes=64)
+        h2 = [keep.tile([P, S], F32, name="h2_%d" % m) for m in range(N // P)]
+
+        def make_z(first, last):
+            places = slice(first, last)
+            entries = slice(first // 16, last // 16)
+            for t in range(PACK):
+                nc.scalar.activation(partner[:, t, places], gained[:, t, :].indirect(n3_list[:, entries]), ACT.Copy)
+            nc.vector.tensor_tensor(
+                z_rounded[:, places, :].rearrange("p (c i) t -> p c t i", i=4),
+                gained[:, :, places].rearrange("p t (c i) -> p c t i", i=4),
+                partner[:, :, places].rearrange("p t (c i) -> p c t i", i=4),
+                ALU.subtract,
+            )
+            nc.vector.quantize_mx(
+                z_codes[:, places].bitcast(FP8X4), z_planes[:, places],
+                z_rounded[:, places, :].rearrange("p j t -> p (j t)"),
+            )
+
+        def multiply_z(half):
+            places = slice(HALF * half, HALF * (half + 1))
+            for m in range(N // P):
+                cols = slice(P * m, P * (m + 1))
+                nc.tensor.matmul_mx(
+                    h_banks[half][m][:], lhsT=w_codes[:, 1, cols].bitcast(FP8X4), lhsT_scale=w_planes[:, 1, cols],
+                    rhs=z_codes[:, places].bitcast(FP8X4), rhs_scale=z_planes[:, places],
+                    start=False, stop=True,
+                )
+
+        make_z(0, 128)
+        multiply_z(0)
+        make_z(128, 192)
+        nc.vector.tensor_copy(h2[0][:, :HALF], h_banks[0][0][:])
+        make_z(192, 256)
+        multiply_z(1)
+
+        tiles = range(N // P)
+        pairs = [keep.tile([P, 2, W], F32, name="pair%d" % m) for m in tiles]
+        rb = [keep.tile([P, W], F32, name="rb%d" % m) for m in tiles]
+        radius2 = keep.tile([P, N // P, W], F32, name="radius2")
+        for m in tiles:
+            if m > 0:
+                nc.vector.tensor_copy(h2[m][:, :HALF], h_banks[0][m][:])
+            nc.vector.tensor_copy(h2[m][:, HALF:], h_banks[1][m][:])
+            nc.scalar.activation(pairs[m][:, 0, :], h2[m][:].indirect(n4_list[:]), ACT.Copy)
+            nc.scalar.activation(pairs[m][:, 1, :], h2[m][:].indirect(n5_list[:]), ACT.Copy)
+        for m in tiles:
+            nc.vector.scalar_tensor_tensor(rb[m][:], pairs[m][:, 0, :], -0.5, pairs[m][:, 1, :], ALU.mult, ALU.add)
+            squares = keep.tile([P, 2, W], F32, name="squares%d" % m)
+            nc.vector.tensor_tensor(squares[:], pairs[m][:], pairs[m][:], ALU.mult)
+            nc.vector.scalar_tensor_tensor(radius2[:, m, :], squares[:, 0, :], 0.25, squares[:, 1, :], ALU.add, ALU.add)
+
+        ra = keep.tile([P, N // P, W], F32, name="ra")
+        results = [keep.tile([P, S], F32, name="result%d" % m) for m in tiles]
+
+        def put_rb(m):
+            nc.scalar.activation(results[m][:].indirect(n5_list[:]), rb[m][:], ACT.Copy)
+
+        put_rb(0)
+        put_rb(1)
+        nc.scalar.activation(ra[:], radius2[:], ACT.Sqrt)
+        for m in tiles:
+            if m + 2 in tiles:
+                put_rb(m + 2)
+            nc.scalar.activation(results[m][:].indirect(n4_list[:]), ra[:, m, :], ACT.Copy)
+            nc.sync.dma_start(out[P * m : P * (m + 1), :], results[m][:])

@@ -69,6 +69,10 @@ def tile_picked_xhznhsndminpolar_none_p_kernel(
             for r in range(4):
                 queue.dma_start(planes[r:P:32, :].bitcast(I32), picked[8 * r : P : 32, :].bitcast(I32))
 
+        warm = keep.tile([P, 2], F32, name="warm")
+        nc.gpsimd.memset(warm[:, 0:1], 1.0)
+        nc.scalar.activation(warm[:, 1:2], warm[:, 0:1], ACT.Sqrt)
+
         s_planes = keep.tile([P, H + S], U8, name="s_planes", align_bytes=64)
         nc.gpsimd.memset(s_planes[:].bitcast(I32), 0)
         hz_planes = keep.tile([P, S], U8, name="hz_planes", align_bytes=64)

@@ -55,9 +55,9 @@ def tile_picked_xhznhsndminpolar_none_p_kernel(
         n1_list = load_list(n1, "n1_list")
         n2_list = load_list(n2, "n2_list")
         n3_list = load_list(n3, "n3_list")
-        d_table = keep.tile([P, G], U32, name="d_table", tag="big_words", align_bytes=64)
+        d_table = keep.tile([P, G], U32, name="d_table", align_bytes=64)
         nc.sync.dma_start(d_table[:].bitcast(I32), words_of(d_words))
-        x_table = keep.tile([P, T], U32, name="x_table", align_bytes=64)
+        x_table = keep.tile([P, T], U32, name="x_table", tag="big_words", align_bytes=64)
         nc.sync.dma_start(x_table[:].bitcast(I32), words_of(x_words))
         hz_list = load_list(hz, "hz_list")
         n4_list = load_list(n4, "n4_list")
@@ -65,41 +65,58 @@ def tile_picked_xhznhsndminpolar_none_p_kernel(
         gain = keep.tile([P, PACK], F32, name="gain")
         nc.gpsimd.dma_start(gain[:], gn.rearrange("(p t) o -> p (t o)", t=PACK))
 
-        def move_scale_rows(queue, planes, picked):
+        def move_scale_rows(queues, planes, picked):
             for r in range(4):
-                queue.dma_start(planes[r:P:32, :].bitcast(I32), picked[8 * r : P : 32, :].bitcast(I32))
+                queues[r % len(queues)].dma_start(planes[r:P:32, :].bitcast(I32), picked[8 * r : P : 32, :].bitcast(I32))
 
         warm = keep.tile([P, 2], F32, name="warm")
         nc.gpsimd.memset(warm[:, 0:1], 1.0)
         nc.scalar.activation(warm[:, 1:2], warm[:, 0:1], ACT.Sqrt)
 
-        s_planes = keep.tile([P, H + S], U8, name="s_planes", align_bytes=64)
+        s_planes = keep.tile([P, H + S], U8, name="s_planes", tag="s_planes", align_bytes=64)
         nc.gpsimd.memset(s_planes[:].bitcast(I32), 0)
         hz_planes = keep.tile([P, S], U8, name="hz_planes", align_bytes=64)
         nc.gpsimd.memset(hz_planes[:].bitcast(I32), 0)
-        s_picked = keep.tile([P, H + S], U8, name="s_picked", tag="picked_bytes", align_bytes=64)
+        s_picked = keep.tile([P, H + S], U8, name="s_picked", align_bytes=64)
         nc.vector.tensor_copy(s_picked[:, H:], x_bytes[:].indirect(offs_list[:]))
         nc.vector.tensor_copy(s_picked[:, :H].rearrange("p (t m) -> p m t", t=PACK), d_bytes[:].indirect(ci_list[:]))
-        move_scale_rows(nc.scalar, s_planes, s_picked)
+        move_scale_rows([nc.scalar], s_planes, s_picked)
 
-        d_codes = keep.tile([P, H], U32, name="d_codes", align_bytes=64)
+        d_codes = keep.tile([P, H], U32, name="d_codes", tag="d_codes", align_bytes=64)
         nc.vector.tensor_copy(d_codes[:].rearrange("p (t m) -> p m t", t=PACK), d_table[:].indirect(ci_list[:]))
-        x_codes = keep.tile([P, S], U32, name="x_codes", align_bytes=64)
-        nc.vector.tensor_copy(x_codes[:], x_table[:].indirect(offs_list[:]))
+        x_codes = keep.tile([P, S], U32, name="x_codes", tag="x_codes", align_bytes=64)
+        halves = [slice(0, HALF), slice(HALF, S)]
+        list_halves = [slice(0, HALF // 16), slice(HALF // 16, S // 16)]
+        for half in range(2):
+            nc.vector.tensor_copy(x_codes[:, halves[half]], x_table[:].indirect(offs_list[:, list_halves[half]]))
 
         scores = [keep.tile([P, GATHER_COLS], F32, name="scores%d" % t) for t in range(PACK)]
-        for t in range(PACK):
-            nc.gpsimd.memset(scores[t][:, S:], 0.0)
-            bank = psum.tile([P, S], F32, name="s_bank%d" % t, tag="bank%d" % t)
+        def score(t, places, tag):
+            width = places.stop - places.start
+            bank = psum.tile([P, width], F32, name="s_" + tag, tag=tag)
             cols = slice(P * t, P * (t + 1))
             nc.tensor.matmul_mx(
                 bank[:], lhsT=d_codes[:, cols].bitcast(FP8X4), lhsT_scale=s_planes[:, cols],
-                rhs=x_codes[:].bitcast(FP8X4), rhs_scale=s_planes[:, H:], start=True, stop=True,
+                rhs=x_codes[:, places].bitcast(FP8X4), rhs_scale=s_planes[:, H + places.start : H + places.stop],
+                start=True, stop=True,
             )
-            nc.vector.tensor_scalar(scores[t][:, :S], bank[:], 0.0625, None, ALU.mult)
+            nc.vector.tensor_scalar(scores[t][:, places], bank[:], 0.0625, None, ALU.mult)
+
+        for t in range(PACK):
+            nc.gpsimd.memset(scores[t][:, S:], 0.0)
+        score(0, halves[0], "bank0")
+        score(0, halves[1], "bank4")
+        for t in range(1, PACK):
+            score(t, slice(0, S), "bank%d" % t)
+
+        hz_picked = keep.tile([P, S], U8, name="hz_picked", tag="s_planes", align_bytes=64)
+        nc.vector.tensor_copy(hz_picked[:], x_bytes[:].indirect(hz_list[:]))
+        move_scale_rows([nc.sync], hz_planes, hz_picked)
+        hz_codes = keep.tile([P, S], U32, name="hz_codes", tag="x_codes", align_bytes=64)
+        nc.vector.tensor_copy(hz_codes[:], x_table[:].indirect(hz_list[:]))
 
         w_codes = keep.tile([P, 2, N], U32, name="w_codes", tag="big_words", align_bytes=64)
-        w_planes = keep.tile([P, 2, N], U8, name="w_planes", tag="picked_bytes", align_bytes=64)
+        w_planes = keep.tile([P, 2, N], U8, name="w_planes", tag="d_codes", align_bytes=64)
         nc.gpsimd.memset(w_planes[:].rearrange("p a n -> p (a n)").bitcast(I32), 0)
         for a, (words, scales) in enumerate(((w2_words, w2_scales), (w1_words, w1_scales))):
             nc.sync.dma_start(w_codes[:, a, :].bitcast(I32), words_of(words))
@@ -108,34 +125,39 @@ def tile_picked_xhznhsndminpolar_none_p_kernel(
                     w_planes[32 * q : 32 * q + 4, a, :].bitcast(I32), scales[0, 4 * q : 4 * q + 4, :].bitcast(I32)
                 )
 
-        hz_picked = keep.tile([P, S], U8, name="hz_picked", align_bytes=64)
-        nc.vector.tensor_copy(hz_picked[:], x_bytes[:].indirect(hz_list[:]))
-        move_scale_rows(nc.sync, hz_planes, hz_picked)
-        hz_codes = keep.tile([P, S], U32, name="hz_codes", align_bytes=64)
-        nc.vector.tensor_copy(hz_codes[:], x_table[:].indirect(hz_list[:]))
-
         gained = keep.tile([P, PACK, S], F32, name="gained")
         for t in range(PACK):
             sent = keep.tile([P, SCATTER_COLS], F32, name="sent%d" % t)
-            nc.scalar.activation(sent[:].indirect(n1_list[:]), scores[t][:, :S], ACT.Copy)
             fetched = keep.tile([P, S], F32, name="fetched%d" % t)
-            nc.scalar.activation(fetched[:], scores[t][:].indirect(n2_list[:]), ACT.Copy)
+            if t == 0:
+                nc.scalar.activation(sent[:].indirect(n1_list[:, list_halves[0]]), scores[t][:, halves[0]], ACT.Copy)
+                nc.scalar.activation(fetched[:], scores[t][:].indirect(n2_list[:]), ACT.Copy)
+                nc.scalar.activation(sent[:].indirect(n1_list[:, list_halves[1]]), scores[t][:, halves[1]], ACT.Copy)
+            else:
+                nc.scalar.activation(sent[:].indirect(n1_list[:]), scores[t][:, :S], ACT.Copy)
+                nc.scalar.activation(fetched[:], scores[t][:].indirect(n2_list[:]), ACT.Copy)
             least = keep.tile([P, S], F32, name="least%d" % t)
             nc.vector.tensor_tensor(least[:], sent[:, :S], fetched[:], ALU.min)
             nc.vector.tensor_scalar(gained[:, t, :], least[:], gain[:, t : t + 1], None, ALU.mult)
 
-        h_banks = [
-            [psum.tile([P, HALF], F32, name="h_bank%d_%d" % (half, m), tag="bank%d" % (4 * (1 - half) + m)) for m in range(N // P)]
-            for half in range(2)
-        ]
+        tiles = range(N // P)
+        h_banks = [psum.tile([P, S], F32, name="h_bank%d" % m, tag="bank%d" % (4 + m)) for m in tiles]
+        early_bank = psum.tile([P, HALF], F32, name="early_bank", tag="bank0")
+
+        def h_out(m, half):
+            return early_bank[:] if (m, half) == (0, 0) else h_banks[m][:, halves[half]]
+
+        def hz_pass(target, m, places):
+            cols = slice(P * m, P * (m + 1))
+            nc.tensor.matmul_mx(
+                target, lhsT=w_codes[:, 0, cols].bitcast(FP8X4), lhsT_scale=w_planes[:, 0, cols],
+                rhs=hz_codes[:, places].bitcast(FP8X4), rhs_scale=hz_planes[:, places], start=True, stop=False,
+            )
+
         for half in range(2):
-            places = slice(HALF * half, HALF * (half + 1))
-            for m in range(N // P):
-                cols = slice(P * m, P * (m + 1))
-                nc.tensor.matmul_mx(
-                    h_banks[half][m][:], lhsT=w_codes[:, 0, cols].bitcast(FP8X4), lhsT_scale=w_planes[:, 0, cols],
-                    rhs=hz_codes[:, places].bitcast(FP8X4), rhs_scale=hz_planes[:, places], start=True, stop=False,
-                )
+            hz_pass(h_out(0, half), 0, halves[half])
+        for m in tiles[1:]:
+            hz_pass(h_banks[m][:], m, slice(0, S))
 
         partner = keep.tile([P, PACK, S], F32, name="partner")
         z_rounded = keep.tile([P, S, PACK], BF16, name="z_rounded", align_bytes=64)
@@ -154,36 +176,34 @@ def tile_picked_xhznhsndminpolar_none_p_kernel(
                 partner[:, :, places].rearrange("p t (c i) -> p c t i", i=4),
                 ALU.subtract,
             )
+
+        def multiply_z(half):
+            places = halves[half]
             nc.vector.quantize_mx(
                 z_codes[:, places].bitcast(FP8X4), z_planes[:, places],
                 z_rounded[:, places, :].rearrange("p j t -> p (j t)"),
             )
-
-        def multiply_z(half):
-            places = slice(HALF * half, HALF * (half + 1))
             for m in range(N // P):
                 cols = slice(P * m, P * (m + 1))
                 nc.tensor.matmul_mx(
-                    h_banks[half][m][:], lhsT=w_codes[:, 1, cols].bitcast(FP8X4), lhsT_scale=w_planes[:, 1, cols],
+                    h_out(m, half), lhsT=w_codes[:, 1, cols].bitcast(FP8X4), lhsT_scale=w_planes[:, 1, cols],
                     rhs=z_codes[:, places].bitcast(FP8X4), rhs_scale=z_planes[:, places],
-                    start=False, stop=True,
+                    start=False, stop=(m == 0 or half == 1),
                 )
 
         make_z(0, 128)
         multiply_z(0)
         make_z(128, 192)
-        nc.vector.tensor_copy(h2[0][:, :HALF], h_banks[0][0][:])
+        nc.vector.tensor_copy(h2[0][:, :HALF], early_bank[:])
         make_z(192, 256)
         multiply_z(1)
 
-        tiles = range(N // P)
         pairs = [keep.tile([P, 2, W], F32, name="pair%d" % m) for m in tiles]
         rb = [keep.tile([P, W], F32, name="rb%d" % m) for m in tiles]
         radius2 = keep.tile([P, N // P, W], F32, name="radius2")
         for m in tiles:
-            if m > 0:
-                nc.vector.tensor_copy(h2[m][:, :HALF], h_banks[0][m][:])
-            nc.vector.tensor_copy(h2[m][:, HALF:], h_banks[1][m][:])
+            late = halves[1] if m == 0 else slice(0, S)
+            nc.vector.tensor_copy(h2[m][:, late], h_banks[m][:, late])
             nc.scalar.activation(pairs[m][:, 0, :], h2[m][:].indirect(n4_list[:]), ACT.Copy)
             nc.scalar.activation(pairs[m][:, 1, :], h2[m][:].indirect(n5_list[:]), ACT.Copy)
         for m in tiles:
@@ -205,4 +225,4 @@ def tile_picked_xhznhsndminpolar_none_p_kernel(
             if m + 2 in tiles:
                 put_rb(m + 2)
             nc.scalar.activation(results[m][:].indirect(n4_list[:]), ra[:, m, :], ACT.Copy)
-            nc.sync.dma_start(out[P * m : P * (m + 1), :], results[m][:])
+            (nc.scalar if m == 3 else nc.sync).dma_start(out[P * m : P * (m + 1), :], results[m][:])

from contextlib import ExitStack

import concourse.mybir as mybir

K, T, S, N, G, H, W = 512, 1024, 256, 512, 2048, 512, 128
FLOPS = 3 * 2 * 512 * 512 * 256

F32 = mybir.dt.float32
BF16 = mybir.dt.bfloat16
I32 = mybir.dt.int32
U32 = mybir.dt.uint32
U16 = mybir.dt.uint16
U8 = mybir.dt.uint8
FP8X4 = mybir.dt.float8_e4m3fn_x4
ALU = mybir.AluOpType
ACT = mybir.ActivationFunctionType

P = 128
PACK = 4
HALF = S // 2
GATHER_COLS = S + 8
SCATTER_COLS = S + 96


def tile_picked_xhznhsndminpolar_none_p_kernel(
    tc, x_words, x_scales, d_words, d_scales, gn, w1_words, w1_scales, w2_words, w2_scales,
    offs, ci, n1, n2, n3, hz, n4, n5, out,
):
    nc = tc.nc

    def words_of(table):
        return table[0].rearrange("p n r -> p (n r)").bitcast(I32)

    with ExitStack() as ctx:
        lists = ctx.enter_context(tc.tile_pool(name="lists", bufs=1))
        keep = ctx.enter_context(tc.tile_pool(name="keep", bufs=1))
        psum = ctx.enter_context(tc.psum_pool(name="psum", bufs=1))

        def load_list(source, name):
            tile = lists.tile(list(source.shape), U16, name=name)
            nc.sync.dma_start(tile[:], source)
            return tile

        x_bytes = keep.tile([P, T], U8, name="x_bytes", align_bytes=64)
        d_bytes = keep.tile([P, G], U8, name="d_bytes", align_bytes=64)

        def load_scale_rows(tile, scales):
            rows = scales[0].bitcast(I32)
            nc.sync.dma_start(tile[:].bitcast(I32), rows.unsqueeze(1).to_broadcast([16, 8, rows.shape[1]]))

        offs_list = load_list(offs, "offs_list")
        load_scale_rows(x_bytes, x_scales)
        ci_list = load_list(ci, "ci_list")
        load_scale_rows(d_bytes, d_scales)
        n1_list = load_list(n1, "n1_list")
        n2_list = load_list(n2, "n2_list")
        n3_list = load_list(n3, "n3_list")
        d_table = keep.tile([P, G], U32, name="d_table", align_bytes=64)
        nc.sync.dma_start(d_table[:].bitcast(I32), words_of(d_words))
        x_table = keep.tile([P, T], U32, name="x_table", tag="big_words", align_bytes=64)
        nc.sync.dma_start(x_table[:].bitcast(I32), words_of(x_words))
        hz_list = load_list(hz, "hz_list")
        n4_list = load_list(n4, "n4_list")
        n5_list = load_list(n5, "n5_list")
        gain = keep.tile([P, PACK], F32, name="gain")
        nc.gpsimd.dma_start(gain[:], gn.rearrange("(p t) o -> p (t o)", t=PACK))

        def move_scale_rows(queues, planes, picked):
            for r in range(4):
                queues[r % len(queues)].dma_start(planes[r:P:32, :].bitcast(I32), picked[8 * r : P : 32, :].bitcast(I32))

        warm = keep.tile([P, 2], F32, name="warm")
        nc.gpsimd.memset(warm[:, 0:1], 1.0)
        nc.scalar.activation(warm[:, 1:2], warm[:, 0:1], ACT.Sqrt)

        s_planes = keep.tile([P, H + S], U8, name="s_planes", tag="s_planes", align_bytes=64)
        nc.gpsimd.memset(s_planes[:].bitcast(I32), 0)
        hz_planes = keep.tile([P, S], U8, name="hz_planes", align_bytes=64)
        nc.gpsimd.memset(hz_planes[:].bitcast(I32), 0)
        s_picked = keep.tile([P, H + S], U8, name="s_picked", align_bytes=64)
        nc.vector.tensor_copy(s_picked[:, H:], x_bytes[:].indirect(offs_list[:]))
        nc.vector.tensor_copy(s_picked[:, :H].rearrange("p (t m) -> p m t", t=PACK), d_bytes[:].indirect(ci_list[:]))
        move_scale_rows([nc.scalar], s_planes, s_picked)

        d_codes = keep.tile([P, H], U32, name="d_codes", tag="d_codes", align_bytes=64)
        nc.vector.tensor_copy(d_codes[:].rearrange("p (t m) -> p m t", t=PACK), d_table[:].indirect(ci_list[:]))
        x_codes = keep.tile([P, S], U32, name="x_codes", tag="x_codes", align_bytes=64)
        halves = [slice(0, HALF), slice(HALF, S)]
        list_halves = [slice(0, HALF // 16), slice(HALF // 16, S // 16)]
        for half in range(2):
            nc.vector.tensor_copy(x_codes[:, halves[half]], x_table[:].indirect(offs_list[:, list_halves[half]]))

        scores = [keep.tile([P, GATHER_COLS], F32, name="scores%d" % t) for t in range(PACK)]
        def score(t, places, tag):
            width = places.stop - places.start
            bank = psum.tile([P, width], F32, name="s_" + tag, tag=tag)
            cols = slice(P * t, P * (t + 1))
            nc.tensor.matmul_mx(
                bank[:], lhsT=d_codes[:, cols].bitcast(FP8X4), lhsT_scale=s_planes[:, cols],
                rhs=x_codes[:, places].bitcast(FP8X4), rhs_scale=s_planes[:, H + places.start : H + places.stop],
                start=True, stop=True,
            )
            nc.vector.tensor_scalar(scores[t][:, places], bank[:], 0.0625, None, ALU.mult)

        for t in range(PACK):
            nc.gpsimd.memset(scores[t][:, S:], 0.0)
        score(0, halves[0], "bank0")
        score(0, halves[1], "bank4")
        for t in range(1, PACK):
            score(t, slice(0, S), "bank%d" % t)

        hz_picked = keep.tile([P, S], U8, name="hz_picked", tag="s_planes", align_bytes=64)
        nc.vector.tensor_copy(hz_picked[:], x_bytes[:].indirect(hz_list[:]))
        move_scale_rows([nc.sync], hz_planes, hz_picked)
        hz_codes = keep.tile([P, S], U32, name="hz_codes", tag="x_codes", align_bytes=64)
        nc.vector.tensor_copy(hz_codes[:], x_table[:].indirect(hz_list[:]))

        w_codes = keep.tile([P, 2, N], U32, name="w_codes", tag="big_words", align_bytes=64)
        w_planes = keep.tile([P, 2, N], U8, name="w_planes", tag="d_codes", align_bytes=64)
        nc.gpsimd.memset(w_planes[:].rearrange("p a n -> p (a n)").bitcast(I32), 0)
        for a, (words, scales) in enumerate(((w2_words, w2_scales), (w1_words, w1_scales))):
            nc.sync.dma_start(w_codes[:, a, :].bitcast(I32), words_of(words))
            for q in range(4):
                nc.sync.dma_start(
                    w_planes[32 * q : 32 * q + 4, a, :].bitcast(I32), scales[0, 4 * q : 4 * q + 4, :].bitcast(I32)
                )

        gained = keep.tile([P, PACK, S], F32, name="gained")
        for t in range(PACK):
            sent = keep.tile([P, SCATTER_COLS], F32, name="sent%d" % t)
            fetched = keep.tile([P, S], F32, name="fetched%d" % t)
            if t == 0:
                nc.scalar.activation(sent[:].indirect(n1_list[:, list_halves[0]]), scores[t][:, halves[0]], ACT.Copy)
                nc.scalar.activation(fetched[:], scores[t][:].indirect(n2_list[:]), ACT.Copy)
                nc.scalar.activation(sent[:].indirect(n1_list[:, list_halves[1]]), scores[t][:, halves[1]], ACT.Copy)
            else:
                nc.scalar.activation(sent[:].indirect(n1_list[:]), scores[t][:, :S], ACT.Copy)
                nc.scalar.activation(fetched[:], scores[t][:].indirect(n2_list[:]), ACT.Copy)
            least = keep.tile([P, S], F32, name="least%d" % t)
            nc.vector.tensor_tensor(least[:], sent[:, :S], fetched[:], ALU.min)
            nc.vector.tensor_scalar(gained[:, t, :], least[:], gain[:, t : t + 1], None, ALU.mult)

        tiles = range(N // P)
        h_banks = [psum.tile([P, S], F32, name="h_bank%d" % m, tag="bank%d" % (4 + m)) for m in tiles]
        early_bank = psum.tile([P, HALF], F32, name="early_bank", tag="bank0")

        def h_out(m, half):
            return early_bank[:] if (m, half) == (0, 0) else h_banks[m][:, halves[half]]

        def hz_pass(target, m, places):
            cols = slice(P * m, P * (m + 1))
            nc.tensor.matmul_mx(
                target, lhsT=w_codes[:, 0, cols].bitcast(FP8X4), lhsT_scale=w_planes[:, 0, cols],
                rhs=hz_codes[:, places].bitcast(FP8X4), rhs_scale=hz_planes[:, places], start=True, stop=False,
            )

        for half in range(2):
            hz_pass(h_out(0, half), 0, halves[half])
        for m in tiles[1:]:
            hz_pass(h_banks[m][:], m, slice(0, S))

        partner = keep.tile([P, PACK, S], F32, name="partner")
        z_rounded = keep.tile([P, S, PACK], BF16, name="z_rounded", align_bytes=64)
        z_codes = keep.tile([P, S], U32, name="z_codes", align_bytes=64)
        z_planes = keep.tile([P, S], U8, name="z_planes", align_bytes=64)
        h2 = [keep.tile([P, S], F32, name="h2_%d" % m) for m in range(N // P)]

        def make_z(first, last):
            places = slice(first, last)
            entries = slice(first // 16, last // 16)
            for t in range(PACK):
                nc.scalar.activation(partner[:, t, places], gained[:, t, :].indirect(n3_list[:, entries]), ACT.Copy)
            nc.vector.tensor_tensor(
                z_rounded[:, places, :].rearrange("p (c i) t -> p c t i", i=4),
                gained[:, :, places].rearrange("p t (c i) -> p c t i", i=4),
                partner[:, :, places].rearrange("p t (c i) -> p c t i", i=4),
                ALU.subtract,
            )

        def multiply_z(half):
            places = halves[half]
            nc.vector.quantize_mx(
                z_codes[:, places].bitcast(FP8X4), z_planes[:, places],
                z_rounded[:, places, :].rearrange("p j t -> p (j t)"),
            )
            for m in range(N // P):
                cols = slice(P * m, P * (m + 1))
                nc.tensor.matmul_mx(
                    h_out(m, half), lhsT=w_codes[:, 1, cols].bitcast(FP8X4), lhsT_scale=w_planes[:, 1, cols],
                    rhs=z_codes[:, places].bitcast(FP8X4), rhs_scale=z_planes[:, places],
                    start=False, stop=(m == 0 or half == 1),
                )

        make_z(0, 128)
        multiply_z(0)
        make_z(128, 192)
        nc.vector.tensor_copy(h2[0][:, :HALF], early_bank[:])
        make_z(192, 256)
        multiply_z(1)

        pairs = [keep.tile([P, 2, W], F32, name="pair%d" % m) for m in tiles]
        rb = [keep.tile([P, W], F32, name="rb%d" % m) for m in tiles]
        radius2 = keep.tile([P, N // P, W], F32, name="radius2")
        for m in tiles:
            late = halves[1] if m == 0 else slice(0, S)
            nc.vector.tensor_copy(h2[m][:, late], h_banks[m][:, late])
            nc.scalar.activation(pairs[m][:, 0, :], h2[m][:].indirect(n4_list[:]), ACT.Copy)
            nc.scalar.activation(pairs[m][:, 1, :], h2[m][:].indirect(n5_list[:]), ACT.Copy)
        for m in tiles:
            nc.vector.scalar_tensor_tensor(rb[m][:], pairs[m][:, 0, :], -0.5, pairs[m][:, 1, :], ALU.mult, ALU.add)
            squares = keep.tile([P, 2, W], F32, name="squares%d" % m)
            nc.vector.tensor_tensor(squares[:], pairs[m][:], pairs[m][:], ALU.mult)
            nc.vector.scalar_tensor_tensor(radius2[:, m, :], squares[:, 0, :], 0.25, squares[:, 1, :], ALU.add, ALU.add)

        ra = keep.tile([P, N // P, W], F32, name="ra")
        results = [keep.tile([P, S], F32, name="result%d" % m) for m in tiles]

        def put_rb(m):
            nc.scalar.activation(results[m][:].indirect(n5_list[:]), rb[m][:], ACT.Copy)

        put_rb(0)
        put_rb(1)
        nc.scalar.activation(ra[:], radius2[:], ACT.Sqrt)
        for m in tiles:
            if m + 2 in tiles:
                put_rb(m + 2)
            nc.scalar.activation(results[m][:].indirect(n4_list[:]), ra[:, m, :], ACT.Copy)
            (nc.scalar if m == 3 else nc.sync).dma_start(out[P * m : P * (m + 1), :], results[m][:])
